import numpy as np, ml_dtypes
CORES = [4,20,60,84,92,100,116]
N = 7
import mx_ref
NC, ROOT = 128, 4
A = np.float32(0.0125)
BF = ml_dtypes.bfloat16
def cut(t, i, w=512):
    return t[:, w * i:w * i + w]
def tile(rs):
    return np.stack(rs, axis=2).reshape(128, -1).astype(BF)
def setup_inputs(rng):
    def f(*shape):
        return mx_ref.flush((rng.standard_normal(shape, dtype=np.float32) * np.exp2(rng.integers(-2, 3, shape[:-1] + (1,)))).astype(BF))
    return {"q": f(N, 128, 4 * NC), "k": f(N, 128, 4 * 512), "v": f(N, 128, 512)}
def setup_inputs_blocks(rng):
    d = setup_inputs(rng)
    for k in ("v",): d[k] = mx_ref.spread(d[k], rng, 4)
    for k in ("q", "k"): d[k] = mx_ref.spread(d[k], rng, 1)
    return d
def setup_inputs_wide(rng):
    d = setup_inputs(rng)
    for k in ("v",): d[k] = mx_ref.flush((d[k].astype(np.float32) * np.exp2(rng.integers(-8, 9, (N, 1, 1))).astype(np.float32)).astype(BF))
    return d
def setup_inputs_sharp(rng):
    d = setup_inputs(rng); v = d["q"].astype(np.float32).reshape(N, 128, -1, 4)
    d["q"] = mx_ref.flush((v * np.exp2(rng.integers(-2, 4, (N, 1, v.shape[2], 1))).astype(np.float32)).reshape(d["q"].shape).astype(BF))
    return d
def setup_inputs_offset(rng):
    d = setup_inputs(rng); v = d["k"].astype(np.float32).reshape(N, 128, -1, 4)
    d["k"] = mx_ref.flush((v + 12 * rng.standard_normal((1, 128, 1, 4), dtype=np.float32)).reshape(d["k"].shape).astype(BF))
    return d
def reference(q, k, v, own=None):
    ONE = mx_ref.quantize(np.ones((128, 512), BF)); Q = mx_ref.quantize(q[ROOT])
    S = [[mx_ref.matmul(mx_ref.quantize(cut(k[j], b)), Q) * A for b in range(4)] for j in range(N)]
    lo = np.stack([np.max(s, axis=(0, 1))[None] for s in S]); hi = np.broadcast_to(lo.max(axis=0) + 8, lo.shape).copy()
    c = lo if own is None else own["c"]
    p = np.stack([tile([np.exp(np.maximum(s - c[j], -20).astype(np.float64)).astype(np.float32) for s in S[j]]) for j in range(N)])
    use = p if own is None else own["p"]
    e = np.exp((c - c.max(axis=0)).astype(np.float64))[:, 0]; wlo = np.zeros((N, N, NC), np.float32); whi = np.ones((N, N, NC), np.float32); wlo[ROOT] = e * (1 - 4e-5); whi[ROOT] = e * (1 + 4e-5)
    w = np.zeros((N, N, NC), np.float32); w[ROOT] = e
    if own is not None: w = own["w"]
    num = den = 0
    for j in range(N):
        P = mx_ref.quantize(use[j])
        num = num + w[ROOT][j].astype(np.float64) * mx_ref.matmul(mx_ref.quantize(v[j]), P); den = den + w[ROOT][j].astype(np.float64) * mx_ref.matmul(ONE, P)
    o = np.full((N, 128, NC), np.nan, np.float32); o[ROOT] = (num / den).astype(np.float32)
    return {"c": c, "c__lo": lo, "c__hi": hi, "p": p, "w": w, "w__lo": wlo, "w__hi": whi, "o": o}

@@ -1,0 +1,326 @@
+from concourse.bass import DstId, RemoteDMATransfer
+from concourse.mybir import dt, AluOpType, AxisListType, ActivationFunctionType
+
+N = 7
+NQ = 128
+SIM = 128
+W = NQ + 1
+SLOT = 132
+F32, BF, X4, U8 = "float32", "bfloat16", "float8_e4m3fn_x4", "uint8"
+
+SCRATCH = {
+    "qt": ("sbuf", [128, 512], BF), "qc": ("sbuf", [128, 128], X4), "qs": ("sbuf", [128, 128], U8),
+    "kt": ("sbuf", [128, 2048], BF), "kc": ("sbuf", [128, 512], X4), "ks": ("sbuf", [128, 512], U8),
+    "vt": ("sbuf", [128, 512], BF), "zt": ("sbuf", [128, 512], BF), "ot": ("sbuf", [128, 512], BF),
+    "vc": ("sbuf", [128, 256], X4), "vs": ("sbuf", [128, 256], U8),
+    "sT": ("psum", [128, 2048], F32), "sk": ("psum", [128, 2048], F32),
+    "rm": ("sbuf", [128, 4], F32), "rx": ("sbuf", [128, 4], F32), "one32": ("sbuf", [128, 32], F32),
+    "cb": ("sbuf", [128, 32], F32), "ct": ("sbuf", [128, 32], F32),
+    "u2": ("sbuf", [128, 1024], F32), "c2": ("sbuf", [128, 256], F32), "d2": ("sbuf", [128, 1024], F32),
+    "pt": ("sbuf", [128, 512], BF), "pc": ("sbuf", [128, 128], X4), "ps": ("sbuf", [128, 128], U8),
+    "ab": ("sbuf", [128, SLOT], F32), "rel": ("sbuf", [128, SLOT], F32), "relc": ("sbuf", [128, 4], F32),
+    "cl": ("sbuf", [128, 4 * N], F32), "land": ("sbuf", [128, N * SLOT], F32), "tm": ("sbuf", [128, N * SLOT], F32),
+    "nm": ("sbuf", [128, 4], F32), "wv": ("sbuf", [128, 8], F32), "acc": ("sbuf", [128, SLOT], F32),
+    "rc": ("sbuf", [128, 4], F32), "oT": ("sbuf", [128, 128], F32), "ox": ("sbuf", [128, 128], F32),
+    "oy": ("sbuf", [128, 128], F32), "wz": ("sbuf", [128, 128], F32),
+}
+NEV = 64
+SEMAPHORES = (["e%d" % i for i in range(NEV)] + ["aa%d" % j for j in range(N)]
+              + ["qsa", "qca", "rca", "raa", "csa", "ls0", "ls1", "ls2"])
+
+
+def _bits(mask):
+    return bin(mask).count("1")
+
+
+def _plan(T, topo):
+    cores = [int(c) for c in T.cores]
+    root = cores[T.root]
+
+    def helpers(c, dst):
+        return [x for x in range(SIM) if topo.chip(x) == topo.chip(c) and x not in cores and topo.may_write(x, dst)]
+
+    def by_die(cand, home):
+        a = [x for x in cand if topo.die(x) == topo.die(home)]
+        b = [x for x in cand if topo.die(x) != topo.die(home)]
+        out = []
+        for i in range(max(len(a), len(b))):
+            out += a[i:i + 1] + b[i:i + 1]
+        return out
+
+    near = [c for c in cores if c != root and topo.may_write(root, c) and topo.may_write(c, root)]
+    far = [c for c in cores if c != root and c not in near]
+    far.sort(key=lambda c: (topo.mates(topo.chip(c), topo.chip(root)), c))
+    fwd, back = {}, {}
+    if far:
+        ports = by_die([x for x in helpers(root, far[0]) if all(topo.may_write(x, f) for f in far)], root)
+        ports = ports[:len(far)]
+        for p in ports:
+            fwd[p] = []
+        for i, f in enumerate(far):
+            fwd[ports[i % len(ports)]].append(f)
+        for i, f in enumerate(far):
+            cand = by_die(helpers(f, root), f)
+            back[f] = cand[i % 2] if len(cand) > 1 else cand[0]
+    return cores, root, near, far, fwd, back
+
+
+def rank_program(g, core, T, topo):
+    cores, root, near, far, fwd, back = _plan(T, topo)
+    sem = T.sem
+    u8 = dt.uint8
+    MUL, SUB, ADD, MAX = AluOpType.mult, AluOpType.subtract, AluOpType.add, AluOpType.max
+    EXP, IDN = ActivationFunctionType.Exp, ActivationFunctionType.Identity
+
+    def send(out_ap, in_ap, dst, rsem, lsem):
+        rid, pid, _ = topo.addr(dst)
+        m = topo.mask(core, dst)
+        g.remote_dma(out_ap=out_ap, in_ap=in_ap, remote_sem=rsem, local_sem=lsem, pid=pid, routing_id=rid,
+                     dma_engine_mask=m)
+        return _bits(m)
+
+    def fan(ap, dsts, rsem, lsem):
+        m = topo.mask(core, dsts[0])
+        for d in dsts:
+            m &= topo.mask(core, d)
+        ids = [DstId(rid=topo.addr(d)[0], pnc=topo.addr(d)[1]) for d in dsts]
+        g.remote_dma_fused([RemoteDMATransfer(dst_ids=ids, dma_engine_mask=m, remote_sem=rsem, srcs=[ap],
+                                              dsts=[ap for _ in dsts])], local_sem=lsem)
+        return _bits(m)
+
+    q_plane = T.qs[:, 0:128]
+    q_codes = T.qc[:, 0:128].bitcast(u8)
+
+    if core in fwd:
+        n_in = _bits(topo.mask(root, core))
+        g.wait_ge(sem.qsa, n_in)
+        n = fan(q_plane, fwd[core], sem.qsa, sem.ls0)
+        g.wait_ge(sem.qca, n_in)
+        n += fan(q_codes, fwd[core], sem.qca, sem.ls0)
+        g.wait_ge(sem.ls0, n)
+        return
+
+    for f in far:
+        if back[f] == core:
+            j = T.rank_of(f)
+            n_in = _bits(topo.mask(f, core))
+            g.wait_ge(sem.rca, n_in)
+            n = send(T.cl[:, 4 * j:4 * j + 1], T.relc[:, 0:1], root, sem.csa, sem.ls0)
+            g.wait_ge(sem.raa, n_in)
+            n += send(T.land[:, SLOT * j:SLOT * j + W], T.rel[:, 0:W], root, sem["aa%d" % j], sem.ls0)
+            g.wait_ge(sem.ls0, n)
+            return
+
+    rank = T.rank_of(core)
+    if rank is None:
+        return
+    is_root = core == root
+    V, S, PE, SY = g.vector, g.scalar, g.tensor, g.sync
+    cnt = [0]
+
+    def ev():
+        s = sem["e%d" % cnt[0]]
+        cnt[0] += 1
+        return s
+
+    e_ms = ev()
+    fills = [(T.zt[:], 0.0), (T.one32[:], 1.0), (T.c2[:], -20.0), (T.u2[:], -1e29)]
+    if not is_root:
+        fills.append((T.wz[0:N, :], 0.0))
+    for ap, val in fills:
+        V.memset(ap, val).then_inc(e_ms, 1)
+    n_ms = len(fills)
+
+    e_k, e_v, e_q = ev(), ev(), ev()
+    if is_root:
+        e_ql = ev()
+        SY.dma_start(T.qt[:], T.q[:]).then_inc(e_ql, 16)
+        V.wait_ge(e_ql, 16)
+        V.quantize_mx(T.qc[:, 0:128], T.qs[:, 0:128], T.qt[:, 0:512]).then_inc(e_q, 1)
+        g.wait_ge(e_q, 1)
+        n0 = n1 = 0
+        if fwd:
+            hs = list(fwd)
+            n0 += fan(q_plane, hs, sem.qsa, sem.ls0)
+            n0 += fan(q_codes, hs, sem.qca, sem.ls0)
+        if near:
+            n1 += fan(q_plane, near, sem.qsa, sem.ls1)
+            n1 += fan(q_codes, near, sem.qca, sem.ls1)
+        SY.wait_ge(sem.ls0, n0)
+        SY.dma_start(T.kt[:], T.k[:]).then_inc(e_k, 16)
+        SY.dma_start(T.vt[:], T.v[:]).then_inc(e_v, 16)
+    else:
+        SY.dma_start(T.kt[:], T.k[:]).then_inc(e_k, 16)
+        S.dma_start(T.vt[:], T.v[:]).then_inc(e_v, 16)
+
+    e_one, e_kq, e_vq = ev(), ev(), ev()
+    S.wait_ge(e_ms, n_ms)
+    S.activation(T.ot[:], T.zt[:], EXP).then_inc(e_one, 1)
+    V.wait_ge(e_ms, n_ms)
+    V.wait_ge(e_one, 1)
+    V.quantize_mx(T.vc[:, 128:256], T.vs[:, 128:256], T.ot[:, 0:512]).then_inc(e_vq, 1)
+    V.wait_ge(e_k, 16)
+    V.quantize_mx(T.kc[:, 0:512], T.ks[:, 0:512], T.kt[:, 0:2048]).then_inc(e_kq, 1)
+    V.wait_ge(e_v, 16)
+    V.quantize_mx(T.vc[:, 0:128], T.vs[:, 0:128], T.vt[:, 0:512]).then_inc(e_vq, 1)
+
+    PE.wait_ge(e_kq, 1)
+    if is_root:
+        PE.wait_ge(e_q, 1)
+    else:
+        src = root if core in near else [h for h in fwd if core in fwd[h]][0]
+        n_q = _bits(topo.mask(src, core))
+        PE.wait_ge(sem.qsa, n_q)
+        PE.wait_ge(sem.qca, n_q)
+    e_t = [ev() for _ in range(4)]
+    e_s = [ev() for _ in range(4)]
+    for i in range(4):
+        PE.matmul_mx(T.sT[:, 512 * i:512 * i + 128], T.qc[:, 0:128], T.qs[:, 0:128],
+                     T.kc[:, 128 * i:128 * i + 128], T.ks[:, 128 * i:128 * i + 128], True, True).then_inc(e_t[i], 1)
+    for b in range(4):
+        PE.matmul_mx(T.sk[:, 512 * b:512 * b + 128], T.kc[:, 128 * b:128 * b + 128], T.ks[:, 128 * b:128 * b + 128],
+                     T.qc[:, 0:128], T.qs[:, 0:128], True, True).then_inc(e_s[b], 1)
+
+    e_r, e_rx, e_cb, e_ct, e_bc = ev(), ev(), ev(), ev(), ev()
+    for i in range(4):
+        V.wait_ge(e_t[i], 1)
+        V.tensor_reduce(T.rm[:, i:i + 1], T.sT[:, 512 * i:512 * i + 128], axis=AxisListType.X, op=MAX).then_inc(e_r, 1)
+    V.wait_ge(e_r, 4)
+    V.tensor_reduce(T.rx[:, 0:1], T.rm[:, 0:4], axis=AxisListType.X, op=MAX).then_inc(e_rx, 1)
+    V.wait_ge(e_rx, 1)
+    V.tensor_scalar(T.cb[:, 0:32], T.one32[:, 0:32], T.rx[:, 0:1], 0.0125, MUL, MUL).then_inc(e_cb, 1)
+
+    la = lc = 0
+    if not is_root:
+        g.wait_ge(e_cb, 1)
+        if core in near:
+            lc = send(T.cl[:, 4 * rank:4 * rank + 1], T.cb[:, 0:1], root, sem.csa, sem.ls1)
+        else:
+            lc = send(T.relc[:, 0:1], T.cb[:, 0:1], back[core], sem.rca, sem.ls1)
+
+    e_u = [ev() for _ in range(4)]
+    for b in range(4):
+        S.wait_ge(e_s[b], 1)
+        S.activation(T.u2[:, 256 * b + 1:256 * b + 256:2], T.sk[:, 512 * b:512 * b + 128], IDN,
+                     scale=0.0125).then_inc(e_u[b], 1)
+
+    V.wait_ge(e_cb, 1)
+    V.transpose(T.ct[:, 0:32], T.cb[:, 0:32]).then_inc(e_ct, 1)
+    if is_root:
+        e_oc = ev()
+        V.tensor_copy(T.cl[:, 4 * rank:4 * rank + 1], T.cb[:, 0:1]).then_inc(e_oc, 1)
+    V.wait_ge(e_ct, 1)
+    S.wait_ge(e_ct, 1)
+    k = 0
+    for a in range(4):
+        for a2 in range(4):
+            out = T.c2[32 * a2:32 * a2 + 32, 64 * a:64 * a + 64:2]
+            in_ = T.ct[32 * a:32 * a + 32, 0:32]
+            if k % 3 == 2:
+                S.activation(out, in_, IDN).then_inc(e_bc, 1)
+            else:
+                V.tensor_copy(out, in_).then_inc(e_bc, 1)
+            k += 1
+
+    e_d = [ev() for _ in range(4)]
+    e_p, e_pq, e_a = ev(), ev(), ev()
+    V.wait_ge(e_bc, 16)
+    for b in range(4):
+        V.wait_ge(e_u[b], 1)
+        V.tensor_tensor_scan(T.d2[:, 256 * b:256 * b + 256], T.u2[:, 256 * b:256 * b + 256], T.c2[:, 0:256], 0.0,
+                             SUB, MAX).then_inc(e_d[b], 1)
+        S.wait_ge(e_d[b], 1)
+        S.activation(T.pt[:, b:512:4], T.d2[:, 256 * b + 1:256 * b + 256:2], EXP).then_inc(e_p, 1)
+    V.wait_ge(e_p, 4)
+    V.quantize_mx(T.pc[:, 0:128], T.ps[:, 0:128], T.pt[:, 0:512]).then_inc(e_pq, 1)
+
+    PE.wait_ge(e_vq, 2)
+    PE.wait_ge(e_pq, 1)
+    PE.matmul_mx(T.sT[:, 0:256], T.pc[:, 0:128], T.ps[:, 0:128], T.vc[:, 0:256], T.vs[:, 0:256], True,
+                 True).then_inc(e_a, 1)
+
+    e_out = ev()
+    n_out = 0
+    if not is_root:
+        e_ab = ev()
+        V.wait_ge(e_a, 1)
+        V.tensor_copy(T.ab[:, 0:W], T.sT[:, 0:W]).then_inc(e_ab, 1)
+        g.wait_ge(e_ab, 1)
+        if core in near:
+            la = send(T.land[:, SLOT * rank:SLOT * rank + W], T.ab[:, 0:W], root, sem["aa%d" % rank], sem.ls2)
+        else:
+            la = send(T.rel[:, 0:W], T.ab[:, 0:W], back[core], sem.raa, sem.ls2)
+        SY.wait_ge(sem.ls2, la)
+        SY.wait_ge(e_cb, 1)
+        SY.wait_ge(e_p, 4)
+        SY.wait_ge(e_ms, n_ms)
+        SY.dma_start(T.p[:], T.pt[:]).then_inc(e_out, 16)
+        SY.dma_start(T.c[:], T.cb[:, 0:1]).then_inc(e_out, 16)
+        SY.dma_start(T.w[:], T.wz[0:N, :]).then_inc(e_out, 16)
+        SY.wait_ge(e_out, 48)
+        g.wait_ge(sem.ls1, lc)
+        g.wait_ge(sem.ls2, la)
+        return
+
+    SY.wait_ge(e_cb, 1)
+    SY.dma_start(T.c[:], T.cb[:, 0:1]).then_inc(e_out, 16)
+    SY.wait_ge(e_p, 4)
+    SY.dma_start(T.p[:], T.pt[:]).then_inc(e_out, 16)
+    n_out = 32
+
+    others = near + far
+    n_c = 0
+    for c in others:
+        n_c += _bits(topo.mask(c if c in near else back[c], root))
+    e_m, e_w = ev(), ev()
+    V.wait_ge(e_oc, 1)
+    V.wait_ge(sem.csa, n_c)
+    V.tensor_reduce(T.nm[:, 0:1], T.cl[:, 0:4 * N:4], axis=AxisListType.X, op=MAX, negate=True).then_inc(e_m, 1)
+    S.wait_ge(e_m, 1)
+    S.activation(T.wv[:, 0:N], T.cl[:, 0:4 * N:4], EXP, bias=T.nm[:, 0:1]).then_inc(e_w, 1)
+    SY.wait_ge(e_w, 1)
+    for j in range(N):
+        SY.dma_start(T.w[j:j + 1, :], T.wv[:, j:j + 1]).then_inc(e_out, 16)
+        n_out += 16
+
+    e_acc = ev()
+    V.wait_ge(e_w, 1)
+    V.wait_ge(e_a, 1)
+    V.tensor_scalar(T.acc[:, 0:W], T.sT[:, 0:W], T.wv[:, rank:rank + 1], None, MUL).then_inc(e_acc, 1)
+    S.wait_ge(e_w, 1)
+    for c in others:
+        j = T.rank_of(c)
+        e_tm, e_nx = ev(), ev()
+        S.wait_ge(sem["aa%d" % j], _bits(topo.mask(c if c in near else back[c], root)))
+        S.activation(T.tm[:, SLOT * j:SLOT * j + W], T.land[:, SLOT * j:SLOT * j + W], IDN,
+                     scale=T.wv[:, j:j + 1]).then_inc(e_tm, 1)
+        V.wait_ge(e_tm, 1)
+        V.wait_ge(e_acc, 1)
+        V.tensor_tensor(T.acc[:, 0:W], T.acc[:, 0:W], T.tm[:, SLOT * j:SLOT * j + W], ADD).then_inc(e_nx, 1)
+        e_acc = e_nx
+
+    e_rc, e_ot, e_ox, e_oy = ev(), ev(), ev(), ev()
+    V.wait_ge(e_acc, 1)
+    V.reciprocal(T.rc[:, 0:1], T.acc[:, NQ:NQ + 1]).then_inc(e_rc, 1)
+    V.wait_ge(e_rc, 1)
+    V.tensor_scalar(T.oT[:, 0:128], T.acc[:, 0:128], T.rc[:, 0:1], None, MUL).then_inc(e_ot, 1)
+    V.wait_ge(e_ot, 1)
+    V.transpose(T.ox[:, 0:128], T.oT[:, 0:128]).then_inc(e_ox, 1)
+    V.wait_ge(e_ox, 1)
+    S.wait_ge(e_ox, 1)
+    k = 0
+    for a in range(4):
+        for b in range(4):
+            out = T.oy[32 * b:32 * b + 32, 32 * a:32 * a + 32]
+            in_ = T.ox[32 * a:32 * a + 32, 32 * b:32 * b + 32]
+            if k % 2:
+                S.activation(out, in_, IDN).then_inc(e_oy, 1)
+            else:
+                V.tensor_copy(out, in_).then_inc(e_oy, 1)
+            k += 1
+    SY.wait_ge(e_oy, 16)
+    SY.dma_start(T.o[:], T.oy[:]).then_inc(e_out, 16)
+    n_out += 16
+    SY.wait_ge(e_out, n_out)
+    g.wait_ge(sem.ls0, n0)
+    g.wait_ge(sem.ls1, n1)

@@ -18,15 +18,15 @@ SCRATCH = {
     "cb": ("sbuf", [128, 32], F32), "ct": ("sbuf", [128, 32], F32),
     "u2": ("sbuf", [128, 1024], F32), "c2": ("sbuf", [128, 256], F32), "d2": ("sbuf", [128, 1024], F32),
     "pt": ("sbuf", [128, 512], BF), "pc": ("sbuf", [128, 128], X4), "ps": ("sbuf", [128, 128], U8),
-    "ab": ("sbuf", [128, SLOT], F32), "rel": ("sbuf", [128, SLOT], F32), "relc": ("sbuf", [128, 4], F32),
+    "ab": ("sbuf", [128, SLOT], F32),
     "cl": ("sbuf", [128, 4 * N], F32), "land": ("sbuf", [128, N * SLOT], F32), "tm": ("sbuf", [128, N * SLOT], F32),
     "nm": ("sbuf", [128, 4], F32), "wv": ("sbuf", [128, 8], F32), "acc": ("sbuf", [128, SLOT], F32),
     "rc": ("sbuf", [128, 4], F32), "oT": ("sbuf", [128, 128], F32), "ox": ("sbuf", [128, 128], F32),
     "oy": ("sbuf", [128, 128], F32), "wz": ("sbuf", [128, 128], F32),
 }
-NEV = 64
+NEV = 80
 SEMAPHORES = (["e%d" % i for i in range(NEV)] + ["aa%d" % j for j in range(N)]
-              + ["qsa", "qca", "rca", "raa", "csa", "ls0", "ls1", "ls2"])
+              + ["qsa", "qca", "ka", "va", "csa", "ls0", "ls1", "ls2"])
 
 
 def _bits(mask):
@@ -51,7 +51,7 @@ def _plan(T, topo):
     near = [c for c in cores if c != root and topo.may_write(root, c) and topo.may_write(c, root)]
     far = [c for c in cores if c != root and c not in near]
     far.sort(key=lambda c: (topo.mates(topo.chip(c), topo.chip(root)), c))
-    fwd, back = {}, {}
+    fwd, comp = {}, {}
     if far:
         ports = by_die([x for x in helpers(root, far[0]) if all(topo.may_write(x, f) for f in far)], root)
         ports = ports[:len(far)]
@@ -61,12 +61,12 @@ def _plan(T, topo):
             fwd[ports[i % len(ports)]].append(f)
         for i, f in enumerate(far):
             cand = by_die(helpers(f, root), f)
-            back[f] = cand[i % 2] if len(cand) > 1 else cand[0]
-    return cores, root, near, far, fwd, back
+            comp[f] = cand[i % 2] if len(cand) > 1 else cand[0]
+    return cores, root, near, far, fwd, comp
 
 
 def rank_program(g, core, T, topo):
-    cores, root, near, far, fwd, back = _plan(T, topo)
+    cores, root, near, far, fwd, comp = _plan(T, topo)
     sem = T.sem
     u8 = dt.uint8
     MUL, SUB, ADD, MAX = AluOpType.mult, AluOpType.subtract, AluOpType.add, AluOpType.max
@@ -93,28 +93,27 @@ def rank_program(g, core, T, topo):
 
     if core in fwd:
         n_in = _bits(topo.mask(root, core))
+        dsts = [comp[f] for f in fwd[core]]
         g.wait_ge(sem.qsa, n_in)
-        n = fan(q_plane, fwd[core], sem.qsa, sem.ls0)
+        n = fan(q_plane, dsts, sem.qsa, sem.ls0)
         g.wait_ge(sem.qca, n_in)
-        n += fan(q_codes, fwd[core], sem.qca, sem.ls0)
+        n += fan(q_codes, dsts, sem.qca, sem.ls0)
         g.wait_ge(sem.ls0, n)
         return
 
+    owner = None
     for f in far:
-        if back[f] == core:
-            j = T.rank_of(f)
-            n_in = _bits(topo.mask(f, core))
-            g.wait_ge(sem.rca, n_in)
-            n = send(T.cl[:, 4 * j:4 * j + 1], T.relc[:, 0:1], root, sem.csa, sem.ls0)
-            g.wait_ge(sem.raa, n_in)
-            n += send(T.land[:, SLOT * j:SLOT * j + W], T.rel[:, 0:W], root, sem["aa%d" % j], sem.ls0)
-            g.wait_ge(sem.ls0, n)
-            return
-
+        if comp[f] == core:
+            owner = f
     rank = T.rank_of(core)
-    if rank is None:
+    if rank is None and owner is None:
         return
     is_root = core == root
+    is_h = owner is not None
+    is_far = core in far
+    sends = is_h or core in near
+    if is_h:
+        rank = T.rank_of(owner)
     V, S, PE, SY = g.vector, g.scalar, g.tensor, g.sync
     cnt = [0]
 
@@ -125,20 +124,22 @@ def rank_program(g, core, T, topo):
 
     e_ms = ev()
     fills = [(T.zt[:], 0.0), (T.one32[:], 1.0), (T.c2[:], -20.0), (T.u2[:], -1e29)]
-    if not is_root:
+    if not is_root and not is_h:
         fills.append((T.wz[0:N, :], 0.0))
     for ap, val in fills:
         V.memset(ap, val).then_inc(e_ms, 1)
     n_ms = len(fills)
 
-    e_k, e_v, e_q = ev(), ev(), ev()
+    e_v, e_q = ev(), ev()
+    e_k = []
+    n0 = n1 = 0
     if is_root:
         e_ql = ev()
+        e_k = [ev()]
         SY.dma_start(T.qt[:], T.q[:]).then_inc(e_ql, 16)
         V.wait_ge(e_ql, 16)
         V.quantize_mx(T.qc[:, 0:128], T.qs[:, 0:128], T.qt[:, 0:512]).then_inc(e_q, 1)
         g.wait_ge(e_q, 1)
-        n0 = n1 = 0
         if fwd:
             hs = list(fwd)
             n0 += fan(q_plane, hs, sem.qsa, sem.ls0)
@@ -147,29 +148,69 @@ def rank_program(g, core, T, topo):
             n1 += fan(q_plane, near, sem.qsa, sem.ls1)
             n1 += fan(q_codes, near, sem.qca, sem.ls1)
         SY.wait_ge(sem.ls0, n0)
-        SY.dma_start(T.kt[:], T.k[:]).then_inc(e_k, 16)
+        SY.dma_start(T.kt[:], T.k[:]).then_inc(e_k[0], 16)
         SY.dma_start(T.vt[:], T.v[:]).then_inc(e_v, 16)
-    else:
-        SY.dma_start(T.kt[:], T.k[:]).then_inc(e_k, 16)
+    elif is_far:
+        e_k = [ev(), ev()]
+        SY.dma_start(T.kt[:, 0:1024], T.k[:, 0:1024]).then_inc(e_k[0], 16)
+        S.dma_start(T.kt[:, 1024:2048], T.k[:, 1024:2048]).then_inc(e_k[1], 16)
+        SY.dma_start(T.vt[:], T.v[:]).then_inc(e_v, 16)
+    elif not is_h:
+        e_k = [ev()]
+        SY.dma_start(T.kt[:], T.k[:]).then_inc(e_k[0], 16)
         S.dma_start(T.vt[:], T.v[:]).then_inc(e_v, 16)
 
-    e_one, e_kq, e_vq = ev(), ev(), ev()
+    e_one, e_oq, e_vq = ev(), ev(), ev()
+    e_kq = []
     S.wait_ge(e_ms, n_ms)
     S.activation(T.ot[:], T.zt[:], EXP).then_inc(e_one, 1)
     V.wait_ge(e_ms, n_ms)
     V.wait_ge(e_one, 1)
-    V.quantize_mx(T.vc[:, 128:256], T.vs[:, 128:256], T.ot[:, 0:512]).then_inc(e_vq, 1)
-    V.wait_ge(e_k, 16)
-    V.quantize_mx(T.kc[:, 0:512], T.ks[:, 0:512], T.kt[:, 0:2048]).then_inc(e_kq, 1)
-    V.wait_ge(e_v, 16)
-    V.quantize_mx(T.vc[:, 0:128], T.vs[:, 0:128], T.vt[:, 0:512]).then_inc(e_vq, 1)
+    V.quantize_mx(T.vc[:, 128:256], T.vs[:, 128:256], T.ot[:, 0:512]).then_inc(e_oq, 1)
+    if not is_h:
+        wd = 512 // len(e_k)
+        for i in range(len(e_k)):
+            s = ev()
+            e_kq.append(s)
+            V.wait_ge(e_k[i], 16)
+            V.quantize_mx(T.kc[:, wd * i:wd * i + wd], T.ks[:, wd * i:wd * i + wd],
+                          T.kt[:, 4 * wd * i:4 * wd * i + 4 * wd]).then_inc(s, 1)
+        V.wait_ge(e_v, 16)
+        V.quantize_mx(T.vc[:, 0:128], T.vs[:, 0:128], T.vt[:, 0:512]).then_inc(e_vq, 1)
 
-    PE.wait_ge(e_kq, 1)
+    lk = 0
+    if is_far:
+        h = comp[core]
+        for i in range(2):
+            g.wait_ge(e_kq[i], 1)
+            ap = T.kc[:, 256 * i:256 * i + 256].bitcast(u8)
+            lk += send(ap, ap, h, sem.ka, sem.ls0)
+        lk += send(T.ks[:, 0:512], T.ks[:, 0:512], h, sem.ka, sem.ls0)
+        g.wait_ge(e_vq, 1)
+        ap = T.vc[:, 0:128].bitcast(u8)
+        lk += send(ap, ap, h, sem.va, sem.ls0)
+        lk += send(T.vs[:, 0:128], T.vs[:, 0:128], h, sem.va, sem.ls0)
+
+    if is_h:
+        PE.wait_ge(sem.ka, 3 * _bits(topo.mask(owner, core)))
+    else:
+        for s in e_kq:
+            PE.wait_ge(s, 1)
     if is_root:
         PE.wait_ge(e_q, 1)
     else:
-        src = root if core in near else [h for h in fwd if core in fwd[h]][0]
+        if is_h:
+            src = [x for x in fwd if owner in fwd[x]][0]
+        elif is_far:
+            src = comp[core]
+        else:
+            src = root
         n_q = _bits(topo.mask(src, core))
+        if is_h:
+            g.wait_ge(sem.qsa, n_q)
+            lk += send(q_plane, q_plane, owner, sem.qsa, sem.ls0)
+            g.wait_ge(sem.qca, n_q)
+            lk += send(q_codes, q_codes, owner, sem.qca, sem.ls0)
         PE.wait_ge(sem.qsa, n_q)
         PE.wait_ge(sem.qca, n_q)
     e_t = [ev() for _ in range(4)]
@@ -191,12 +232,9 @@ def rank_program(g, core, T, topo):
     V.tensor_scalar(T.cb[:, 0:32], T.one32[:, 0:32], T.rx[:, 0:1], 0.0125, MUL, MUL).then_inc(e_cb, 1)
 
     la = lc = 0
-    if not is_root:
+    if sends:
         g.wait_ge(e_cb, 1)
-        if core in near:
-            lc = send(T.cl[:, 4 * rank:4 * rank + 1], T.cb[:, 0:1], root, sem.csa, sem.ls1)
-        else:
-            lc = send(T.relc[:, 0:1], T.cb[:, 0:1], back[core], sem.rca, sem.ls1)
+        lc = send(T.cl[:, 4 * rank:4 * rank + 1], T.cb[:, 0:1], root, sem.csa, sem.ls1)
 
     e_u = [ev() for _ in range(4)]
     for b in range(4):
@@ -234,7 +272,11 @@ def rank_program(g, core, T, topo):
     V.wait_ge(e_p, 4)
     V.quantize_mx(T.pc[:, 0:128], T.ps[:, 0:128], T.pt[:, 0:512]).then_inc(e_pq, 1)
 
-    PE.wait_ge(e_vq, 2)
+    PE.wait_ge(e_oq, 1)
+    if is_h:
+        PE.wait_ge(sem.va, 2 * _bits(topo.mask(owner, core)))
+    else:
+        PE.wait_ge(e_vq, 1)
     PE.wait_ge(e_pq, 1)
     PE.matmul_mx(T.sT[:, 0:256], T.pc[:, 0:128], T.ps[:, 0:128], T.vc[:, 0:256], T.vs[:, 0:256], True,
                  True).then_inc(e_a, 1)
@@ -242,24 +284,28 @@ def rank_program(g, core, T, topo):
     e_out = ev()
     n_out = 0
     if not is_root:
-        e_ab = ev()
-        V.wait_ge(e_a, 1)
-        V.tensor_copy(T.ab[:, 0:W], T.sT[:, 0:W]).then_inc(e_ab, 1)
-        g.wait_ge(e_ab, 1)
-        if core in near:
+        if sends:
+            e_ab = ev()
+            V.wait_ge(e_a, 1)
+            V.tensor_copy(T.ab[:, 0:W], T.sT[:, 0:W]).then_inc(e_ab, 1)
+            g.wait_ge(e_ab, 1)
             la = send(T.land[:, SLOT * rank:SLOT * rank + W], T.ab[:, 0:W], root, sem["aa%d" % rank], sem.ls2)
+            SY.wait_ge(sem.ls2, la)
         else:
-            la = send(T.rel[:, 0:W], T.ab[:, 0:W], back[core], sem.raa, sem.ls2)
-        SY.wait_ge(sem.ls2, la)
-        SY.wait_ge(e_cb, 1)
-        SY.wait_ge(e_p, 4)
-        SY.wait_ge(e_ms, n_ms)
-        SY.dma_start(T.p[:], T.pt[:]).then_inc(e_out, 16)
-        SY.dma_start(T.c[:], T.cb[:, 0:1]).then_inc(e_out, 16)
-        SY.dma_start(T.w[:], T.wz[0:N, :]).then_inc(e_out, 16)
-        SY.wait_ge(e_out, 48)
-        g.wait_ge(sem.ls1, lc)
-        g.wait_ge(sem.ls2, la)
+            SY.wait_ge(e_a, 1)
+        if not is_h:
+            SY.wait_ge(e_cb, 1)
+            SY.wait_ge(e_p, 4)
+            SY.wait_ge(e_ms, n_ms)
+            SY.dma_start(T.p[:], T.pt[:]).then_inc(e_out, 16)
+            SY.dma_start(T.c[:], T.cb[:, 0:1]).then_inc(e_out, 16)
+            SY.dma_start(T.w[:], T.wz[0:N, :]).then_inc(e_out, 16)
+            SY.wait_ge(e_out, 48)
+        if lk:
+            g.wait_ge(sem.ls0, lk)
+        if sends:
+            g.wait_ge(sem.ls1, lc)
+            g.wait_ge(sem.ls2, la)
         return
 
     SY.wait_ge(e_cb, 1)
@@ -271,7 +317,7 @@ def rank_program(g, core, T, topo):
     others = near + far
     n_c = 0
     for c in others:
-        n_c += _bits(topo.mask(c if c in near else back[c], root))
+        n_c += _bits(topo.mask(c if c in near else comp[c], root))
     e_m, e_w = ev(), ev()
     V.wait_ge(e_oc, 1)
     V.wait_ge(sem.csa, n_c)
@@ -291,7 +337,7 @@ def rank_program(g, core, T, topo):
     for c in others:
         j = T.rank_of(c)
         e_tm, e_nx = ev(), ev()
-        S.wait_ge(sem["aa%d" % j], _bits(topo.mask(c if c in near else back[c], root)))
+        S.wait_ge(sem["aa%d" % j], _bits(topo.mask(c if c in near else comp[c], root)))
         S.activation(T.tm[:, SLOT * j:SLOT * j + W], T.land[:, SLOT * j:SLOT * j + W], IDN,
                      scale=T.wv[:, j:j + 1]).then_inc(e_tm, 1)
         V.wait_ge(e_tm, 1)

@@ -14,7 +14,8 @@ SCRATCH = {
     "vt": ("sbuf", [128, 512], BF), "zt": ("sbuf", [128, 512], BF), "ot": ("sbuf", [128, 512], BF),
     "vc": ("sbuf", [128, 256], X4), "vs": ("sbuf", [128, 256], U8),
     "sT": ("psum", [128, 2048], F32), "sk": ("psum", [128, 2048], F32),
-    "rm": ("sbuf", [128, 4], F32), "rx": ("sbuf", [128, 4], F32), "one32": ("sbuf", [128, 32], F32),
+    "rm": ("sbuf", [128, 4], F32), "ta": ("sbuf", [128, 32], F32), "cs": ("sbuf", [128, 4], F32),
+    "one32": ("sbuf", [128, 32], F32), "al": ("sbuf", [128, 8], F32),
     "cb": ("sbuf", [128, 32], F32), "ct": ("sbuf", [128, 32], F32),
     "u2": ("sbuf", [128, 1024], F32), "c2": ("sbuf", [128, 256], F32), "d2": ("sbuf", [128, 1024], F32),
     "pt": ("sbuf", [128, 512], BF), "pc": ("sbuf", [128, 128], X4), "ps": ("sbuf", [128, 128], U8),
@@ -24,7 +25,7 @@ SCRATCH = {
     "rc": ("sbuf", [128, 4], F32), "oT": ("sbuf", [128, 128], F32), "ox": ("sbuf", [128, 128], F32),
     "oy": ("sbuf", [128, 128], F32), "wz": ("sbuf", [128, 128], F32),
 }
-NEV = 80
+NEV = 110
 SEMAPHORES = (["e%d" % i for i in range(NEV)] + ["aa%d" % j for j in range(N)]
               + ["qsa", "qca", "ka", "va", "csa", "ls0", "ls1", "ls2"])
 
@@ -222,31 +223,48 @@ def rank_program(g, core, T, topo):
         PE.matmul_mx(T.sk[:, 512 * b:512 * b + 128], T.kc[:, 128 * b:128 * b + 128], T.ks[:, 128 * b:128 * b + 128],
                      T.qc[:, 0:128], T.qs[:, 0:128], True, True).then_inc(e_s[b], 1)
 
-    e_r, e_rx, e_cb, e_ct, e_bc = ev(), ev(), ev(), ev(), ev()
-    for i in range(4):
-        V.wait_ge(e_t[i], 1)
-        V.tensor_reduce(T.rm[:, i:i + 1], T.sT[:, 512 * i:512 * i + 128], axis=AxisListType.X, op=MAX).then_inc(e_r, 1)
-    V.wait_ge(e_r, 4)
-    V.tensor_reduce(T.rx[:, 0:1], T.rm[:, 0:4], axis=AxisListType.X, op=MAX).then_inc(e_rx, 1)
-    V.wait_ge(e_rx, 1)
-    V.tensor_scalar(T.cb[:, 0:32], T.one32[:, 0:32], T.rx[:, 0:1], 0.0125, MUL, MUL).then_inc(e_cb, 1)
+    e_r = [ev() for _ in range(4)]
+    e_ta, e_cb, e_cs, e_ct, e_bc = ev(), ev(), ev(), ev(), ev()
 
-    la = lc = 0
-    if sends:
-        g.wait_ge(e_cb, 1)
-        lc = send(T.cl[:, 4 * rank:4 * rank + 1], T.cb[:, 0:1], root, sem.csa, sem.ls1)
+    def red(i):
+        V.wait_ge(e_t[i], 1)
+        V.tensor_reduce(T.rm[:, i:i + 1], T.sT[:, 512 * i:512 * i + 128], axis=AxisListType.X,
+                        op=MAX).then_inc(e_r[i], 1)
+
+    red(0)
+    red(1)
+    red(2)
+    V.wait_ge(e_r[0], 1)
+    V.wait_ge(e_r[1], 1)
+    V.tensor_scalar(T.ta[:, 0:32], T.one32[:, 0:32], T.rm[:, 0:1], T.rm[:, 1:2], MUL, MAX).then_inc(e_ta, 1)
+    red(3)
+    V.wait_ge(e_r[2], 1)
+    V.wait_ge(e_r[3], 1)
+    V.wait_ge(e_ta, 1)
+    V.tensor_scalar(T.cb[:, 0:32], T.ta[:, 0:32], T.rm[:, 2:3], T.rm[:, 3:4], MAX, MAX).then_inc(e_cb, 1)
 
     e_u = [ev() for _ in range(4)]
-    for b in range(4):
+    e_oc = ev()
+
+    def scale_u(b):
         S.wait_ge(e_s[b], 1)
         S.activation(T.u2[:, 256 * b + 1:256 * b + 256:2], T.sk[:, 512 * b:512 * b + 128], IDN,
                      scale=0.0125).then_inc(e_u[b], 1)
 
+    scale_u(0)
+    scale_u(1)
+    S.wait_ge(e_cb, 1)
+    S.activation(T.cs[:, 0:1], T.cb[:, 0:1], IDN, scale=0.0125).then_inc(e_cs, 1)
+    if is_root:
+        S.activation(T.cl[:, 4 * rank:4 * rank + 1], T.cb[:, 0:1], IDN, scale=0.0125).then_inc(e_oc, 1)
+
+    la = lc = 0
+    if sends:
+        g.wait_ge(e_cs, 1)
+        lc = send(T.cl[:, 4 * rank:4 * rank + 1], T.cs[:, 0:1], root, sem.csa, sem.ls1)
+
     V.wait_ge(e_cb, 1)
     V.transpose(T.ct[:, 0:32], T.cb[:, 0:32]).then_inc(e_ct, 1)
-    if is_root:
-        e_oc = ev()
-        V.tensor_copy(T.cl[:, 4 * rank:4 * rank + 1], T.cb[:, 0:1]).then_inc(e_oc, 1)
     V.wait_ge(e_ct, 1)
     S.wait_ge(e_ct, 1)
     k = 0
@@ -254,22 +272,27 @@ def rank_program(g, core, T, topo):
         for a2 in range(4):
             out = T.c2[32 * a2:32 * a2 + 32, 64 * a:64 * a + 64:2]
             in_ = T.ct[32 * a:32 * a + 32, 0:32]
-            if k % 3 == 2:
-                S.activation(out, in_, IDN).then_inc(e_bc, 1)
+            if k % 2:
+                S.activation(out, in_, IDN, scale=0.0125).then_inc(e_bc, 1)
             else:
-                V.tensor_copy(out, in_).then_inc(e_bc, 1)
+                V.tensor_scalar(out, in_, 0.0125, None, MUL).then_inc(e_bc, 1)
             k += 1
+    scale_u(2)
+    scale_u(3)
 
-    e_d = [ev() for _ in range(4)]
+    pieces = [(0, 0, NQ), (1, 0, NQ), (2, 0, NQ), (3, 0, NQ // 2), (3, NQ // 2, NQ)]
+    n_p = len(pieces)
     e_p, e_pq, e_a = ev(), ev(), ev()
     V.wait_ge(e_bc, 16)
-    for b in range(4):
+    for b, t0, t1 in pieces:
+        e_d = ev()
         V.wait_ge(e_u[b], 1)
-        V.tensor_tensor_scan(T.d2[:, 256 * b:256 * b + 256], T.u2[:, 256 * b:256 * b + 256], T.c2[:, 0:256], 0.0,
-                             SUB, MAX).then_inc(e_d[b], 1)
-        S.wait_ge(e_d[b], 1)
-        S.activation(T.pt[:, b:512:4], T.d2[:, 256 * b + 1:256 * b + 256:2], EXP).then_inc(e_p, 1)
-    V.wait_ge(e_p, 4)
+        V.tensor_tensor_scan(T.d2[:, 256 * b + 2 * t0:256 * b + 2 * t1], T.u2[:, 256 * b + 2 * t0:256 * b + 2 * t1],
+                             T.c2[:, 2 * t0:2 * t1], 0.0, SUB, MAX).then_inc(e_d, 1)
+        S.wait_ge(e_d, 1)
+        S.activation(T.pt[:, 4 * t0 + b:4 * t1:4], T.d2[:, 256 * b + 2 * t0 + 1:256 * b + 2 * t1:2],
+                     EXP).then_inc(e_p, 1)
+    V.wait_ge(e_p, n_p)
     V.quantize_mx(T.pc[:, 0:128], T.ps[:, 0:128], T.pt[:, 0:512]).then_inc(e_pq, 1)
 
     PE.wait_ge(e_oq, 1)
@@ -278,28 +301,28 @@ def rank_program(g, core, T, topo):
     else:
         PE.wait_ge(e_vq, 1)
     PE.wait_ge(e_pq, 1)
-    PE.matmul_mx(T.sT[:, 0:256], T.pc[:, 0:128], T.ps[:, 0:128], T.vc[:, 0:256], T.vs[:, 0:256], True,
+    PE.matmul_mx(T.sT[:, 0:NQ + 2], T.pc[:, 0:128], T.ps[:, 0:128], T.vc[:, 0:NQ + 2], T.vs[:, 0:NQ + 2], True,
                  True).then_inc(e_a, 1)
 
     e_out = ev()
     n_out = 0
     if not is_root:
+        if not is_h:
+            SY.wait_ge(e_ms, n_ms)
+            SY.dma_start(T.w[:], T.wz[0:N, :]).then_inc(e_out, 16)
+            SY.wait_ge(e_cs, 1)
+            SY.dma_start(T.c[:], T.cs[:, 0:1]).then_inc(e_out, 16)
+            SY.wait_ge(e_p, n_p)
+            SY.dma_start(T.p[:], T.pt[:]).then_inc(e_out, 16)
         if sends:
             e_ab = ev()
             V.wait_ge(e_a, 1)
             V.tensor_copy(T.ab[:, 0:W], T.sT[:, 0:W]).then_inc(e_ab, 1)
             g.wait_ge(e_ab, 1)
             la = send(T.land[:, SLOT * rank:SLOT * rank + W], T.ab[:, 0:W], root, sem["aa%d" % rank], sem.ls2)
-            SY.wait_ge(sem.ls2, la)
         else:
             SY.wait_ge(e_a, 1)
         if not is_h:
-            SY.wait_ge(e_cb, 1)
-            SY.wait_ge(e_p, 4)
-            SY.wait_ge(e_ms, n_ms)
-            SY.dma_start(T.p[:], T.pt[:]).then_inc(e_out, 16)
-            SY.dma_start(T.c[:], T.cb[:, 0:1]).then_inc(e_out, 16)
-            SY.dma_start(T.w[:], T.wz[0:N, :]).then_inc(e_out, 16)
             SY.wait_ge(e_out, 48)
         if lk:
             g.wait_ge(sem.ls0, lk)
@@ -308,13 +331,18 @@ def rank_program(g, core, T, topo):
             g.wait_ge(sem.ls2, la)
         return
 
-    SY.wait_ge(e_cb, 1)
-    SY.dma_start(T.c[:], T.cb[:, 0:1]).then_inc(e_out, 16)
-    SY.wait_ge(e_p, 4)
+    SY.wait_ge(e_cs, 1)
+    SY.dma_start(T.c[:], T.cs[:, 0:1]).then_inc(e_out, 16)
+    SY.wait_ge(e_p, n_p)
     SY.dma_start(T.p[:], T.pt[:]).then_inc(e_out, 16)
     n_out = 32
 
-    others = near + far
+    def when(c):
+        for i, h in enumerate(fwd):
+            if c in fwd[h]:
+                return i + 2 * fwd[h].index(c)
+
+    others = near + sorted(far, key=when)
     n_c = 0
     for c in others:
         n_c += _bits(topo.mask(c if c in near else comp[c], root))
@@ -329,44 +357,69 @@ def rank_program(g, core, T, topo):
         SY.dma_start(T.w[j:j + 1, :], T.wv[:, j:j + 1]).then_inc(e_out, 16)
         n_out += 16
 
+    HF = NQ // 2
     e_acc = ev()
     V.wait_ge(e_w, 1)
     V.wait_ge(e_a, 1)
     V.tensor_scalar(T.acc[:, 0:W], T.sT[:, 0:W], T.wv[:, rank:rank + 1], None, MUL).then_inc(e_acc, 1)
     S.wait_ge(e_w, 1)
-    for c in others:
+    e_rc = ev()
+    e_hf = [ev(), ev()]
+    lsum, e_l = T.acc[:, NQ:NQ + 1], e_acc
+    for i, c in enumerate(others):
         j = T.rank_of(c)
-        e_tm, e_nx = ev(), ev()
-        S.wait_ge(sem["aa%d" % j], _bits(topo.mask(c if c in near else comp[c], root)))
-        S.activation(T.tm[:, SLOT * j:SLOT * j + W], T.land[:, SLOT * j:SLOT * j + W], IDN,
+        e_tm, e_nx, e_ln = ev(), ev(), ev()
+        last = i == len(others) - 1
+        n_a = _bits(topo.mask(c if c in near else comp[c], root))
+        S.wait_ge(sem["aa%d" % j], n_a)
+        S.activation(T.tm[:, SLOT * j:SLOT * j + NQ], T.land[:, SLOT * j:SLOT * j + NQ], IDN,
                      scale=T.wv[:, j:j + 1]).then_inc(e_tm, 1)
+        V.wait_ge(sem["aa%d" % j], n_a)
+        V.wait_ge(e_l, 1)
+        V.tensor_scalar(T.al[:, i:i + 1], T.land[:, SLOT * j + NQ:SLOT * j + W], T.wv[:, j:j + 1], lsum, MUL,
+                        ADD).then_inc(e_ln, 1)
+        lsum, e_l = T.al[:, i:i + 1], e_ln
+        if last:
+            V.wait_ge(e_l, 1)
+            V.reciprocal(T.rc[:, 0:1], lsum).then_inc(e_rc, 1)
         V.wait_ge(e_tm, 1)
         V.wait_ge(e_acc, 1)
-        V.tensor_tensor(T.acc[:, 0:W], T.acc[:, 0:W], T.tm[:, SLOT * j:SLOT * j + W], ADD).then_inc(e_nx, 1)
-        e_acc = e_nx
+        if last:
+            for h in range(2):
+                V.tensor_tensor(T.acc[:, HF * h:HF * h + HF], T.acc[:, HF * h:HF * h + HF],
+                                T.tm[:, SLOT * j + HF * h:SLOT * j + HF * h + HF], ADD).then_inc(e_hf[h], 1)
+        else:
+            V.tensor_tensor(T.acc[:, 0:NQ], T.acc[:, 0:NQ], T.tm[:, SLOT * j:SLOT * j + NQ], ADD).then_inc(e_nx, 1)
+            e_acc = e_nx
 
-    e_rc, e_ot, e_ox, e_oy = ev(), ev(), ev(), ev()
-    V.wait_ge(e_acc, 1)
-    V.reciprocal(T.rc[:, 0:1], T.acc[:, NQ:NQ + 1]).then_inc(e_rc, 1)
+    e_ot = [ev(), ev()]
+    e_ox = [ev(), ev()]
+    e_oy = [ev(), ev()]
+    V.wait_ge(e_hf[0], 1)
     V.wait_ge(e_rc, 1)
-    V.tensor_scalar(T.oT[:, 0:128], T.acc[:, 0:128], T.rc[:, 0:1], None, MUL).then_inc(e_ot, 1)
-    V.wait_ge(e_ot, 1)
-    V.transpose(T.ox[:, 0:128], T.oT[:, 0:128]).then_inc(e_ox, 1)
-    V.wait_ge(e_ox, 1)
-    S.wait_ge(e_ox, 1)
-    k = 0
-    for a in range(4):
-        for b in range(4):
-            out = T.oy[32 * b:32 * b + 32, 32 * a:32 * a + 32]
-            in_ = T.ox[32 * a:32 * a + 32, 32 * b:32 * b + 32]
-            if k % 2:
-                S.activation(out, in_, IDN).then_inc(e_oy, 1)
-            else:
-                V.tensor_copy(out, in_).then_inc(e_oy, 1)
-            k += 1
-    SY.wait_ge(e_oy, 16)
-    SY.dma_start(T.o[:], T.oy[:]).then_inc(e_out, 16)
-    n_out += 16
+    S.wait_ge(e_hf[1], 1)
+    S.wait_ge(e_rc, 1)
+    V.tensor_scalar(T.oT[:, 0:HF], T.acc[:, 0:HF], T.rc[:, 0:1], None, MUL).then_inc(e_ot[0], 1)
+    S.activation(T.oT[:, HF:NQ], T.acc[:, HF:NQ], IDN, scale=T.rc[:, 0:1]).then_inc(e_ot[1], 1)
+    for h in range(2):
+        V.wait_ge(e_ot[h], 1)
+        V.transpose(T.ox[:, HF * h:HF * h + HF], T.oT[:, HF * h:HF * h + HF]).then_inc(e_ox[h], 1)
+    for h in range(2):
+        V.wait_ge(e_ox[h], 1)
+        S.wait_ge(e_ox[h], 1)
+        k = 0
+        for b in (2 * h, 2 * h + 1):
+            for a in range(4):
+                out = T.oy[32 * b:32 * b + 32, 32 * a:32 * a + 32]
+                in_ = T.ox[32 * a:32 * a + 32, 32 * b:32 * b + 32]
+                if k % 2:
+                    S.activation(out, in_, IDN).then_inc(e_oy[h], 1)
+                else:
+                    V.tensor_copy(out, in_).then_inc(e_oy[h], 1)
+                k += 1
+        SY.wait_ge(e_oy[h], 8)
+        SY.dma_start(T.o[HF * h:HF * h + HF, :], T.oy[HF * h:HF * h + HF, :]).then_inc(e_out, 16)
+        n_out += 16
     SY.wait_ge(e_out, n_out)
     g.wait_ge(sem.ls0, n0)
     g.wait_ge(sem.ls1, n1)

from concourse.bass import DstId, RemoteDMATransfer
from concourse.mybir import dt, AluOpType, AxisListType, ActivationFunctionType

N = 7
NQ = 128
SIM = 128
W = NQ + 1
SLOT = 132
F32, BF, X4, U8 = "float32", "bfloat16", "float8_e4m3fn_x4", "uint8"

SCRATCH = {
    "qt": ("sbuf", [128, 512], BF), "qc": ("sbuf", [128, 128], X4), "qs": ("sbuf", [128, 128], U8),
    "kt": ("sbuf", [128, 2048], BF), "kc": ("sbuf", [128, 512], X4), "ks": ("sbuf", [128, 512], U8),
    "vt": ("sbuf", [128, 512], BF), "zt": ("sbuf", [128, 512], BF), "ot": ("sbuf", [128, 512], BF),
    "vc": ("sbuf", [128, 256], X4), "vs": ("sbuf", [128, 256], U8),
    "sT": ("psum", [128, 2048], F32), "sk": ("psum", [128, 2048], F32),
    "rm": ("sbuf", [128, 4], F32), "ta": ("sbuf", [128, 32], F32), "cs": ("sbuf", [128, 4], F32),
    "one32": ("sbuf", [128, 32], F32), "al": ("sbuf", [128, 8], F32),
    "cb": ("sbuf", [128, 32], F32), "ct": ("sbuf", [128, 32], F32),
    "u2": ("sbuf", [128, 1024], F32), "c2": ("sbuf", [128, 256], F32), "d2": ("sbuf", [128, 1024], F32),
    "pt": ("sbuf", [128, 512], BF), "pc": ("sbuf", [128, 128], X4), "ps": ("sbuf", [128, 128], U8),
    "ab": ("sbuf", [128, SLOT], F32),
    "cl": ("sbuf", [128, 4 * N], F32), "land": ("sbuf", [128, N * SLOT], F32), "tm": ("sbuf", [128, N * SLOT], F32),
    "nm": ("sbuf", [128, 4], F32), "wv": ("sbuf", [128, 8], F32), "acc": ("sbuf", [128, SLOT], F32),
    "rc": ("sbuf", [128, 4], F32), "oT": ("sbuf", [128, 128], F32), "ox": ("sbuf", [128, 128], F32),
    "oy": ("sbuf", [128, 128], F32), "wz": ("sbuf", [128, 128], F32),
}
NEV = 110
SEMAPHORES = (["e%d" % i for i in range(NEV)] + ["aa%d" % j for j in range(N)]
              + ["qsa", "qca", "ka", "va", "csa", "ls0", "ls1", "ls2"])


def _bits(mask):
    return bin(mask).count("1")


def _plan(T, topo):
    cores = [int(c) for c in T.cores]
    root = cores[T.root]

    def helpers(c, dst):
        return [x for x in range(SIM) if topo.chip(x) == topo.chip(c) and x not in cores and topo.may_write(x, dst)]

    def by_die(cand, home):
        a = [x for x in cand if topo.die(x) == topo.die(home)]
        b = [x for x in cand if topo.die(x) != topo.die(home)]
        out = []
        for i in range(max(len(a), len(b))):
            out += a[i:i + 1] + b[i:i + 1]
        return out

    near = [c for c in cores if c != root and topo.may_write(root, c) and topo.may_write(c, root)]
    far = [c for c in cores if c != root and c not in near]
    far.sort(key=lambda c: (topo.mates(topo.chip(c), topo.chip(root)), c))
    fwd, comp = {}, {}
    if far:
        ports = by_die([x for x in helpers(root, far[0]) if all(topo.may_write(x, f) for f in far)], root)
        ports = ports[:len(far)]
        for p in ports:
            fwd[p] = []
        for i, f in enumerate(far):
            fwd[ports[i % len(ports)]].append(f)
        for i, f in enumerate(far):
            cand = by_die(helpers(f, root), f)
            comp[f] = cand[i % 2] if len(cand) > 1 else cand[0]
    return cores, root, near, far, fwd, comp


def rank_program(g, core, T, topo):
    cores, root, near, far, fwd, comp = _plan(T, topo)
    sem = T.sem
    u8 = dt.uint8
    MUL, SUB, ADD, MAX = AluOpType.mult, AluOpType.subtract, AluOpType.add, AluOpType.max
    EXP, IDN = ActivationFunctionType.Exp, ActivationFunctionType.Identity

    def send(out_ap, in_ap, dst, rsem, lsem):
        rid, pid, _ = topo.addr(dst)
        m = topo.mask(core, dst)
        g.remote_dma(out_ap=out_ap, in_ap=in_ap, remote_sem=rsem, local_sem=lsem, pid=pid, routing_id=rid,
                     dma_engine_mask=m)
        return _bits(m)

    def fan(ap, dsts, rsem, lsem):
        m = topo.mask(core, dsts[0])
        for d in dsts:
            m &= topo.mask(core, d)
        ids = [DstId(rid=topo.addr(d)[0], pnc=topo.addr(d)[1]) for d in dsts]
        g.remote_dma_fused([RemoteDMATransfer(dst_ids=ids, dma_engine_mask=m, remote_sem=rsem, srcs=[ap],
                                              dsts=[ap for _ in dsts])], local_sem=lsem)
        return _bits(m)

    q_plane = T.qs[:, 0:128]
    q_codes = T.qc[:, 0:128].bitcast(u8)

    if core in fwd:
        n_in = _bits(topo.mask(root, core))
        dsts = [comp[f] for f in fwd[core]]
        g.wait_ge(sem.qsa, n_in)
        n = fan(q_plane, dsts, sem.qsa, sem.ls0)
        g.wait_ge(sem.qca, n_in)
        n += fan(q_codes, dsts, sem.qca, sem.ls0)
        g.wait_ge(sem.ls0, n)
        return

    owner = None
    for f in far:
        if comp[f] == core:
            owner = f
    rank = T.rank_of(core)
    if rank is None and owner is None:
        return
    is_root = core == root
    is_h = owner is not None
    is_far = core in far
    sends = is_h or core in near
    if is_h:
        rank = T.rank_of(owner)
    V, S, PE, SY = g.vector, g.scalar, g.tensor, g.sync
    cnt = [0]

    def ev():
        s = sem["e%d" % cnt[0]]
        cnt[0] += 1
        return s

    e_ms = ev()
    fills = [(T.zt[:], 0.0), (T.one32[:], 1.0), (T.c2[:], -20.0), (T.u2[:], -1e29)]
    if not is_root and not is_h:
        fills.append((T.wz[0:N, :], 0.0))
    for ap, val in fills:
        V.memset(ap, val).then_inc(e_ms, 1)
    n_ms = len(fills)

    e_v, e_q = ev(), ev()
    e_k = []
    n0 = n1 = 0
    if is_root:
        e_ql = ev()
        e_k = [ev()]
        SY.dma_start(T.qt[:], T.q[:]).then_inc(e_ql, 16)
        V.wait_ge(e_ql, 16)
        V.quantize_mx(T.qc[:, 0:128], T.qs[:, 0:128], T.qt[:, 0:512]).then_inc(e_q, 1)
        g.wait_ge(e_q, 1)
        if fwd:
            hs = list(fwd)
            n0 += fan(q_plane, hs, sem.qsa, sem.ls0)
            n0 += fan(q_codes, hs, sem.qca, sem.ls0)
        if near:
            n1 += fan(q_plane, near, sem.qsa, sem.ls1)
            n1 += fan(q_codes, near, sem.qca, sem.ls1)
        SY.wait_ge(sem.ls0, n0)
        SY.dma_start(T.kt[:], T.k[:]).then_inc(e_k[0], 16)
        SY.dma_start(T.vt[:], T.v[:]).then_inc(e_v, 16)
    elif is_far:
        e_k = [ev(), ev()]
        SY.dma_start(T.kt[:, 0:1024], T.k[:, 0:1024]).then_inc(e_k[0], 16)
        S.dma_start(T.kt[:, 1024:2048], T.k[:, 1024:2048]).then_inc(e_k[1], 16)
        SY.dma_start(T.vt[:], T.v[:]).then_inc(e_v, 16)
    elif not is_h:
        e_k = [ev()]
        SY.dma_start(T.kt[:], T.k[:]).then_inc(e_k[0], 16)
        S.dma_start(T.vt[:], T.v[:]).then_inc(e_v, 16)

    e_one, e_oq, e_vq = ev(), ev(), ev()
    e_kq = []
    S.wait_ge(e_ms, n_ms)
    S.activation(T.ot[:], T.zt[:], EXP).then_inc(e_one, 1)
    V.wait_ge(e_ms, n_ms)
    V.wait_ge(e_one, 1)
    V.quantize_mx(T.vc[:, 128:256], T.vs[:, 128:256], T.ot[:, 0:512]).then_inc(e_oq, 1)
    if not is_h:
        wd = 512 // len(e_k)
        for i in range(len(e_k)):
            s = ev()
            e_kq.append(s)
            V.wait_ge(e_k[i], 16)
            V.quantize_mx(T.kc[:, wd * i:wd * i + wd], T.ks[:, wd * i:wd * i + wd],
                          T.kt[:, 4 * wd * i:4 * wd * i + 4 * wd]).then_inc(s, 1)
        V.wait_ge(e_v, 16)
        V.quantize_mx(T.vc[:, 0:128], T.vs[:, 0:128], T.vt[:, 0:512]).then_inc(e_vq, 1)

    lk = 0
    if is_far:
        h = comp[core]
        for i in range(2):
            g.wait_ge(e_kq[i], 1)
            ap = T.kc[:, 256 * i:256 * i + 256].bitcast(u8)
            lk += send(ap, ap, h, sem.ka, sem.ls0)
        lk += send(T.ks[:, 0:512], T.ks[:, 0:512], h, sem.ka, sem.ls0)
        g.wait_ge(e_vq, 1)
        ap = T.vc[:, 0:128].bitcast(u8)
        lk += send(ap, ap, h, sem.va, sem.ls0)
        lk += send(T.vs[:, 0:128], T.vs[:, 0:128], h, sem.va, sem.ls0)

    if is_h:
        PE.wait_ge(sem.ka, 3 * _bits(topo.mask(owner, core)))
    else:
        for s in e_kq:
            PE.wait_ge(s, 1)
    if is_root:
        PE.wait_ge(e_q, 1)
    else:
        if is_h:
            src = [x for x in fwd if owner in fwd[x]][0]
        elif is_far:
            src = comp[core]
        else:
            src = root
        n_q = _bits(topo.mask(src, core))
        if is_h:
            g.wait_ge(sem.qsa, n_q)
            lk += send(q_plane, q_plane, owner, sem.qsa, sem.ls0)
            g.wait_ge(sem.qca, n_q)
            lk += send(q_codes, q_codes, owner, sem.qca, sem.ls0)
        PE.wait_ge(sem.qsa, n_q)
        PE.wait_ge(sem.qca, n_q)
    e_t = [ev() for _ in range(4)]
    e_s = [ev() for _ in range(4)]
    for i in range(4):
        PE.matmul_mx(T.sT[:, 512 * i:512 * i + 128], T.qc[:, 0:128], T.qs[:, 0:128],
                     T.kc[:, 128 * i:128 * i + 128], T.ks[:, 128 * i:128 * i + 128], True, True).then_inc(e_t[i], 1)
    for b in range(4):
        PE.matmul_mx(T.sk[:, 512 * b:512 * b + 128], T.kc[:, 128 * b:128 * b + 128], T.ks[:, 128 * b:128 * b + 128],
                     T.qc[:, 0:128], T.qs[:, 0:128], True, True).then_inc(e_s[b], 1)

    e_r = [ev() for _ in range(4)]
    e_ta, e_cb, e_cs, e_ct, e_bc = ev(), ev(), ev(), ev(), ev()

    def red(i):
        V.wait_ge(e_t[i], 1)
        V.tensor_reduce(T.rm[:, i:i + 1], T.sT[:, 512 * i:512 * i + 128], axis=AxisListType.X,
                        op=MAX).then_inc(e_r[i], 1)

    red(0)
    red(1)
    red(2)
    V.wait_ge(e_r[0], 1)
    V.wait_ge(e_r[1], 1)
    V.tensor_scalar(T.ta[:, 0:32], T.one32[:, 0:32], T.rm[:, 0:1], T.rm[:, 1:2], MUL, MAX).then_inc(e_ta, 1)
    red(3)
    V.wait_ge(e_r[2], 1)
    V.wait_ge(e_r[3], 1)
    V.wait_ge(e_ta, 1)
    V.tensor_scalar(T.cb[:, 0:32], T.ta[:, 0:32], T.rm[:, 2:3], T.rm[:, 3:4], MAX, MAX).then_inc(e_cb, 1)

    e_u = [ev() for _ in range(4)]
    e_oc = ev()

    def scale_u(b):
        S.wait_ge(e_s[b], 1)
        S.activation(T.u2[:, 256 * b + 1:256 * b + 256:2], T.sk[:, 512 * b:512 * b + 128], IDN,
                     scale=0.0125).then_inc(e_u[b], 1)

    scale_u(0)
    scale_u(1)
    S.wait_ge(e_cb, 1)
    S.activation(T.cs[:, 0:1], T.cb[:, 0:1], IDN, scale=0.0125).then_inc(e_cs, 1)
    if is_root:
        S.activation(T.cl[:, 4 * rank:4 * rank + 1], T.cb[:, 0:1], IDN, scale=0.0125).then_inc(e_oc, 1)

    la = lc = 0
    if sends:
        g.wait_ge(e_cs, 1)
        lc = send(T.cl[:, 4 * rank:4 * rank + 1], T.cs[:, 0:1], root, sem.csa, sem.ls1)

    V.wait_ge(e_cb, 1)
    V.transpose(T.ct[:, 0:32], T.cb[:, 0:32]).then_inc(e_ct, 1)
    V.wait_ge(e_ct, 1)
    S.wait_ge(e_ct, 1)
    k = 0
    for a in range(4):
        for a2 in range(4):
            out = T.c2[32 * a2:32 * a2 + 32, 64 * a:64 * a + 64:2]
            in_ = T.ct[32 * a:32 * a + 32, 0:32]
            if k % 2:
                S.activation(out, in_, IDN, scale=0.0125).then_inc(e_bc, 1)
            else:
                V.tensor_scalar(out, in_, 0.0125, None, MUL).then_inc(e_bc, 1)
            k += 1
    scale_u(2)
    scale_u(3)

    pieces = [(0, 0, NQ), (1, 0, NQ), (2, 0, NQ), (3, 0, NQ // 2), (3, NQ // 2, NQ)]
    n_p = len(pieces)
    e_p, e_pq, e_a = ev(), ev(), ev()
    V.wait_ge(e_bc, 16)
    for b, t0, t1 in pieces:
        e_d = ev()
        V.wait_ge(e_u[b], 1)
        V.tensor_tensor_scan(T.d2[:, 256 * b + 2 * t0:256 * b + 2 * t1], T.u2[:, 256 * b + 2 * t0:256 * b + 2 * t1],
                             T.c2[:, 2 * t0:2 * t1], 0.0, SUB, MAX).then_inc(e_d, 1)
        S.wait_ge(e_d, 1)
        S.activation(T.pt[:, 4 * t0 + b:4 * t1:4], T.d2[:, 256 * b + 2 * t0 + 1:256 * b + 2 * t1:2],
                     EXP).then_inc(e_p, 1)
    V.wait_ge(e_p, n_p)
    V.quantize_mx(T.pc[:, 0:128], T.ps[:, 0:128], T.pt[:, 0:512]).then_inc(e_pq, 1)

    PE.wait_ge(e_oq, 1)
    if is_h:
        PE.wait_ge(sem.va, 2 * _bits(topo.mask(owner, core)))
    else:
        PE.wait_ge(e_vq, 1)
    PE.wait_ge(e_pq, 1)
    PE.matmul_mx(T.sT[:, 0:NQ + 2], T.pc[:, 0:128], T.ps[:, 0:128], T.vc[:, 0:NQ + 2], T.vs[:, 0:NQ + 2], True,
                 True).then_inc(e_a, 1)

    e_out = ev()
    n_out = 0
    if not is_root:
        if not is_h:
            SY.wait_ge(e_ms, n_ms)
            SY.dma_start(T.w[:], T.wz[0:N, :]).then_inc(e_out, 16)
            SY.wait_ge(e_cs, 1)
            SY.dma_start(T.c[:], T.cs[:, 0:1]).then_inc(e_out, 16)
            SY.wait_ge(e_p, n_p)
            SY.dma_start(T.p[:], T.pt[:]).then_inc(e_out, 16)
        if sends:
            e_ab = ev()
            V.wait_ge(e_a, 1)
            V.tensor_copy(T.ab[:, 0:W], T.sT[:, 0:W]).then_inc(e_ab, 1)
            g.wait_ge(e_ab, 1)
            la = send(T.land[:, SLOT * rank:SLOT * rank + W], T.ab[:, 0:W], root, sem["aa%d" % rank], sem.ls2)
        else:
            SY.wait_ge(e_a, 1)
        if not is_h:
            SY.wait_ge(e_out, 48)
        if lk:
            g.wait_ge(sem.ls0, lk)
        if sends:
            g.wait_ge(sem.ls1, lc)
            g.wait_ge(sem.ls2, la)
        return

    SY.wait_ge(e_cs, 1)
    SY.dma_start(T.c[:], T.cs[:, 0:1]).then_inc(e_out, 16)
    SY.wait_ge(e_p, n_p)
    SY.dma_start(T.p[:], T.pt[:]).then_inc(e_out, 16)
    n_out = 32

    def when(c):
        for i, h in enumerate(fwd):
            if c in fwd[h]:
                return i + 2 * fwd[h].index(c)

    others = near + sorted(far, key=when)
    n_c = 0
    for c in others:
        n_c += _bits(topo.mask(c if c in near else comp[c], root))
    e_m, e_w = ev(), ev()
    V.wait_ge(e_oc, 1)
    V.wait_ge(sem.csa, n_c)
    V.tensor_reduce(T.nm[:, 0:1], T.cl[:, 0:4 * N:4], axis=AxisListType.X, op=MAX, negate=True).then_inc(e_m, 1)
    S.wait_ge(e_m, 1)
    S.activation(T.wv[:, 0:N], T.cl[:, 0:4 * N:4], EXP, bias=T.nm[:, 0:1]).then_inc(e_w, 1)
    SY.wait_ge(e_w, 1)
    for j in range(N):
        SY.dma_start(T.w[j:j + 1, :], T.wv[:, j:j + 1]).then_inc(e_out, 16)
        n_out += 16

    HF = NQ // 2
    e_acc = ev()
    V.wait_ge(e_w, 1)
    V.wait_ge(e_a, 1)
    V.tensor_scalar(T.acc[:, 0:W], T.sT[:, 0:W], T.wv[:, rank:rank + 1], None, MUL).then_inc(e_acc, 1)
    S.wait_ge(e_w, 1)
    e_rc = ev()
    e_hf = [ev(), ev()]
    lsum, e_l = T.acc[:, NQ:NQ + 1], e_acc
    for i, c in enumerate(others):
        j = T.rank_of(c)
        e_tm, e_nx, e_ln = ev(), ev(), ev()
        last = i == len(others) - 1
        n_a = _bits(topo.mask(c if c in near else comp[c], root))
        S.wait_ge(sem["aa%d" % j], n_a)
        S.activation(T.tm[:, SLOT * j:SLOT * j + NQ], T.land[:, SLOT * j:SLOT * j + NQ], IDN,
                     scale=T.wv[:, j:j + 1]).then_inc(e_tm, 1)
        V.wait_ge(sem["aa%d" % j], n_a)
        V.wait_ge(e_l, 1)
        V.tensor_scalar(T.al[:, i:i + 1], T.land[:, SLOT * j + NQ:SLOT * j + W], T.wv[:, j:j + 1], lsum, MUL,
                        ADD).then_inc(e_ln, 1)
        lsum, e_l = T.al[:, i:i + 1], e_ln
        if last:
            V.wait_ge(e_l, 1)
            V.reciprocal(T.rc[:, 0:1], lsum).then_inc(e_rc, 1)
        V.wait_ge(e_tm, 1)
        V.wait_ge(e_acc, 1)
        if last:
            for h in range(2):
                V.tensor_tensor(T.acc[:, HF * h:HF * h + HF], T.acc[:, HF * h:HF * h + HF],
                                T.tm[:, SLOT * j + HF * h:SLOT * j + HF * h + HF], ADD).then_inc(e_hf[h], 1)
        else:
            V.tensor_tensor(T.acc[:, 0:NQ], T.acc[:, 0:NQ], T.tm[:, SLOT * j:SLOT * j + NQ], ADD).then_inc(e_nx, 1)
            e_acc = e_nx

    e_ot = [ev(), ev()]
    e_ox = [ev(), ev()]
    e_oy = [ev(), ev()]
    V.wait_ge(e_hf[0], 1)
    V.wait_ge(e_rc, 1)
    S.wait_ge(e_hf[1], 1)
    S.wait_ge(e_rc, 1)
    V.tensor_scalar(T.oT[:, 0:HF], T.acc[:, 0:HF], T.rc[:, 0:1], None, MUL).then_inc(e_ot[0], 1)
    S.activation(T.oT[:, HF:NQ], T.acc[:, HF:NQ], IDN, scale=T.rc[:, 0:1]).then_inc(e_ot[1], 1)
    for h in range(2):
        V.wait_ge(e_ot[h], 1)
        V.transpose(T.ox[:, HF * h:HF * h + HF], T.oT[:, HF * h:HF * h + HF]).then_inc(e_ox[h], 1)
    for h in range(2):
        V.wait_ge(e_ox[h], 1)
        S.wait_ge(e_ox[h], 1)
        k = 0
        for b in (2 * h, 2 * h + 1):
            for a in range(4):
                out = T.oy[32 * b:32 * b + 32, 32 * a:32 * a + 32]
                in_ = T.ox[32 * a:32 * a + 32, 32 * b:32 * b + 32]
                if k % 2:
                    S.activation(out, in_, IDN).then_inc(e_oy[h], 1)
                else:
                    V.tensor_copy(out, in_).then_inc(e_oy[h], 1)
                k += 1
        SY.wait_ge(e_oy[h], 8)
        SY.dma_start(T.o[HF * h:HF * h + HF, :], T.oy[HF * h:HF * h + HF, :]).then_inc(e_out, 16)
        n_out += 16
    SY.wait_ge(e_out, n_out)
    g.wait_ge(sem.ls0, n0)
    g.wait_ge(sem.ls1, n1)
